import numpy as np
import ml_dtypes


def mxq(x, axis, fmt="e4m3"):
    dtype, down = {"e4m3": (ml_dtypes.float8_e4m3fn, 7), "e5m2": (ml_dtypes.float8_e5m2, 14)}[fmt]
    v = np.moveaxis(np.asarray(x, np.float32).astype(ml_dtypes.bfloat16).astype(np.float64), axis, -1)
    blocks = v.reshape(v.shape[:-1] + (-1, 32))
    amax = np.abs(blocks).max(-1, keepdims=True)
    byte = np.maximum(np.where(amax > 0, np.frexp(amax)[1] - 1 + 127, 0) - down, 1)
    scale = np.exp2(byte - 127.0)
    codes = (blocks / scale).astype(np.float32).astype(dtype).astype(np.float64)
    return np.moveaxis((codes * scale).reshape(v.shape), -1, axis)


WIDE = False


def mx_kscale(k, group=512):
    if not WIDE:
        return np.ones(k)
    levels = np.array([18, -18])
    if group != 512:
        return np.exp2(np.random.permutation(np.resize(levels, k // group))).repeat(group)
    if k % 512:
        return np.exp2(np.random.permutation(np.resize(levels, k // 32))).repeat(32)
    a = np.empty((k // 512, 16))
    for p in range(k // 512):
        a[p, :8] = np.random.permutation(np.resize(levels, 8))
        for g in range(8):
            far = levels[np.abs(levels - a[p, g]) >= 10]
            a[p, g + 8] = far[np.random.randint(len(far))]
    return np.exp2(a.ravel()).repeat(32)


def f64(x):
    return np.asarray(x).astype(np.float64)


G, D, I, Q, E = 8, 128, 128, 128, 128


def sgn(shape):
    return np.random.uniform(0.5, 2.0, shape) * np.where(np.random.standard_normal(shape) < 0, -1.0, 1.0)


def setup_inputs():
    n = np.random.standard_normal
    s_d = mx_kscale(D, 0)
    s_i = mx_kscale(I, 0)
    return {
        "kT": (n((G, D, I)) / np.sqrt(D) / s_d[:, None]).astype(np.float32),
        "qT": (n((G, D, Q)) * s_d[:, None]).astype(np.float32),
        "dk": (np.where(np.arange(I)[:, None] <= np.arange(Q)[None], 0.97 ** (np.arange(Q)[None] - np.arange(I)[:, None]), 0.0)).astype(np.float32),
        "t": (sgn((G, I, 1)) * s_i[:, None]).astype(np.float32),
        "v": ((n((G, I, E))) / s_i[:, None]).astype(np.float32),
    }


def reference(kT, qT, dk, t, v):
    kTq = mxq(f64(kT), 1, "e4m3")
    qTq = mxq(f64(qT), 1, "e4m3")
    z = kTq.transpose(0, 2, 1) @ qTq
    p = z * f64(dk) * f64(t)
    pq = mxq(p, 1, "e4m3")
    vq = mxq(f64(v), 1, "e4m3")
    y = pq.transpose(0, 2, 1) @ vq
    ms = np.mean(np.square(y), axis=-1, keepdims=True)
    o = y / np.sqrt(ms + 1e-05)
    return o

@@ -1,0 +1,223 @@
+from contextlib import ExitStack
+
+import concourse.mybir as mybir
+
+G, D, I, Q, E = 8, 128, 128, 128, 128
+FLOPS = 2 * G * (D * I * Q + I * Q * E)
+
+F32 = mybir.dt.float32
+BF16 = mybir.dt.bfloat16
+I32 = mybir.dt.int32
+U32 = mybir.dt.uint32
+U8 = mybir.dt.uint8
+FP8X4 = mybir.dt.float8_e4m3fn_x4
+ACT = mybir.ActivationFunctionType
+ALU = mybir.AluOpType
+
+P = 128
+ROWS = 32
+PACK = 4
+SIDE = 4
+SETS = G // SIDE
+W = 128
+EPS = 1e-05
+SCALAR_WINDOWS = 3
+
+
+def tile_rows_win_rms_kernel(tc, kT, qT, dk, t, v, out):
+    nc = tc.nc
+
+    def set_rows(x, u):
+        return x.flatten_outer_dims()[u * P * PACK : (u + 1) * P * PACK, :].rearrange("(p j) c -> p j c", j=PACK)
+
+    with ExitStack() as ctx:
+        sb = ctx.enter_context(tc.tile_pool(name="sb", bufs=1))
+        ps = ctx.enter_context(tc.psum_pool(name="ps", bufs=1))
+        ctx.enter_context(tc.manual_schedule())
+
+        def tiles(name, shape, dtype):
+            return [sb.tile(shape, dtype, name="%s%d" % (name, u), align_bytes=64) for u in range(SETS)]
+
+        k_raw = tiles("k_raw", [P, PACK, W], F32)
+        q_raw = tiles("q_raw", [P, PACK, W], F32)
+        v_raw = tiles("v_raw", [P, PACK, W], F32)
+        k_bf = tiles("k_bf", [P, W * PACK], BF16)
+        q_bf = tiles("q_bf", [P, W * PACK], BF16)
+        v_bf = tiles("v_bf", [P, W * PACK], BF16)
+        p_bf = tiles("p_bf", [P, W * PACK], BF16)
+        kq_codes = tiles("kq_codes", [P, 3 * W], U32)
+        kq_scales = tiles("kq_scales", [P, 3 * W], U8)
+        odd_scales = tiles("odd_scales", [P, 3 * W], U8)
+        v_codes = tiles("v_codes", [P, W], U32)
+        v_scales = tiles("v_scales", [P, W], U8)
+        p_codes = tiles("p_codes", [P, W], U32)
+        p_scales = tiles("p_scales", [P, W], U8)
+        dkt = tiles("dkt", [P, PACK, W], F32)
+        z_sb = tiles("z_sb", [P, W, PACK], F32)
+        sq_sum = tiles("sq_sum", [P, SIDE], F32)
+        rstd = tiles("rstd", [P, SIDE], F32)
+        o_sb = tiles("o_sb", [P, SIDE, W], F32)
+        dk_raw = sb.tile([P, PACK, W], F32, name="dk_raw")
+        t_sb = sb.tile([P, SETS, PACK], F32, name="t_sb")
+        squares = sb.tile([P, W], F32, name="squares")
+        warm_in = sb.tile([P, 1], F32, name="warm_in")
+        warm_out = sb.tile([P, 1], F32, name="warm_out")
+        banks = [[ps.tile([P, PACK, W], F32, name="bank%d_%d" % (u, g)) for g in range(SIDE)] for u in range(SETS)]
+
+        def rows(g):
+            return slice(ROWS * g, ROWS * (g + 1))
+
+        def load(dst, x, u):
+            nc.sync.dma_start(out=dst[u][:], in_=set_rows(x, u))
+
+        load(k_raw, kT, 0)
+        load(q_raw, qT, 0)
+        nc.sync.dma_start(out=t_sb[:], in_=t.flatten_outer_dims().rearrange("(u p j) o -> p u (j o)", u=SETS, j=PACK))
+        for g in range(SIDE):
+            nc.sync.dma_start(out=dk_raw[rows(g)], in_=dk.rearrange("(s r) q -> s r q", r=PACK))
+        load(k_raw, kT, 1)
+        load(q_raw, qT, 1)
+        load(v_raw, v, 0)
+        load(v_raw, v, 1)
+
+        nc.vector.memset(warm_in[:], 1.0)
+        nc.scalar.activation(out=warm_out[:], in_=warm_in[:], func=ACT.Abs_reciprocal_sqrt)
+        for u in range(SETS):
+            nc.vector.memset(kq_codes[u][:, 0:W].bitcast(I32), 0)
+            nc.vector.memset(kq_scales[u][:, 0 : 2 * W].bitcast(I32), 0)
+            nc.vector.memset(odd_scales[u][:].bitcast(I32), 0)
+
+        def cast_k(u):
+            nc.vector.tensor_copy(
+                out=k_bf[u][:].rearrange("p (r s j) -> p s r j", r=PACK, j=PACK),
+                in_=k_raw[u][:].rearrange("p j (s r) -> p s r j", r=PACK),
+            )
+
+        def cast(dst, src, u):
+            nc.vector.tensor_copy(
+                out=dst[u][:].rearrange("p (c j) -> p c j", j=PACK), in_=src[u][:].rearrange("p j c -> p c j")
+            )
+
+        def quantize(codes, scales, src):
+            nc.vector.quantize_mx(out=codes.bitcast(FP8X4), scales=scales, in_=src)
+
+        def quantize_k(u):
+            quantize(kq_codes[u][:, W : 2 * W], kq_scales[u][:, W : 2 * W], k_bf[u][:])
+
+        def quantize_q(u):
+            quantize(kq_codes[u][:, 2 * W : 3 * W], kq_scales[u][:, 2 * W : 3 * W], q_bf[u][:])
+
+        def shift_scales(u):
+            nc.vector.tensor_copy(
+                out=odd_scales[u][:, W + ROWS : 2 * W + ROWS].bitcast(I32), in_=kq_scales[u][:, W : 2 * W].bitcast(I32)
+            )
+
+        def scores(u):
+            for step in (0, 2, 1, 3):
+                for g in range(SIDE):
+                    r = (g + step) % PACK
+                    first = W + ROWS * (r - g)
+                    if step % 2 == 0:
+                        k_scales = kq_scales[u][rows(g), first : first + W]
+                    else:
+                        k_scales = odd_scales[u][rows(g), first + ROWS : first + ROWS + W]
+                    nc.tensor.matmul_mx(
+                        out=banks[u][g][:, r, :],
+                        lhsT=kq_codes[u][rows(g), first : first + W].bitcast(FP8X4),
+                        lhsT_scale=k_scales,
+                        rhs=kq_codes[u][rows(g), 2 * W : 3 * W].bitcast(FP8X4),
+                        rhs_scale=kq_scales[u][rows(g), 2 * W : 3 * W],
+                        start=True,
+                        stop=True,
+                    )
+
+        def weights(u):
+            for r in range(PACK):
+                nc.scalar.activation(out=dkt[u][:, r, :], in_=dk_raw[:, r, :], func=ACT.Copy, scale=t_sb[:, u, r : r + 1])
+
+        def scalar_scores_out(u):
+            for g in range(SCALAR_WINDOWS):
+                nc.scalar.copy(out=z_sb[u][rows(g)], in_=banks[u][g][rows(g)].rearrange("p r q -> p q r"))
+
+        def weigh(u, part, z):
+            nc.vector.tensor_tensor(
+                out=p_bf[u][part].rearrange("p (q r) -> p q r", r=PACK),
+                in0=z,
+                in1=dkt[u][part].rearrange("p r q -> p q r"),
+                op=ALU.mult,
+            )
+
+        def weigh_from_psum(u):
+            for g in range(SCALAR_WINDOWS, SIDE):
+                weigh(u, rows(g), banks[u][g][rows(g)].rearrange("p r q -> p q r"))
+
+        def weigh_from_sbuf(u):
+            part = slice(0, ROWS * SCALAR_WINDOWS)
+            weigh(u, part, z_sb[u][part])
+
+        def values(u):
+            for g in range(SIDE):
+                nc.tensor.matmul_mx(
+                    out=banks[u][g][:, 0, :],
+                    lhsT=p_codes[u][rows(g), :].bitcast(FP8X4),
+                    lhsT_scale=p_scales[u][rows(g), :],
+                    rhs=v_codes[u][rows(g), :].bitcast(FP8X4),
+                    rhs_scale=v_scales[u][rows(g), :],
+                    start=True,
+                    stop=True,
+                )
+
+        def norms(u, lo, hi):
+            for g in range(lo, hi):
+                nc.scalar.activation(
+                    out=squares[:], in_=banks[u][g][:, 0, :], func=ACT.Square, accum_out=sq_sum[u][:, g : g + 1]
+                )
+            nc.scalar.activation(
+                out=rstd[u][:, lo:hi], in_=sq_sum[u][:, lo:hi], func=ACT.Abs_reciprocal_sqrt, scale=1.0 / E, bias=EPS
+            )
+
+        def finish(u, lo, hi):
+            for g in range(lo, hi):
+                nc.vector.tensor_scalar(
+                    out=o_sb[u][:, g, :],
+                    in0=banks[u][g][:, 0, :],
+                    scalar1=rstd[u][:, g : g + 1],
+                    scalar2=None,
+                    op0=ALU.mult,
+                )
+            nc.sync.dma_start(out=out[SIDE * u + lo : SIDE * u + hi].rearrange("g q e -> q g e"), in_=o_sb[u][:, lo:hi, :])
+
+        cast_k(0)
+        cast(q_bf, q_raw, 0)
+        quantize_k(0)
+        quantize_q(0)
+        shift_scales(0)
+        scores(0)
+        weights(0)
+        weights(1)
+        cast_k(1)
+        scalar_scores_out(0)
+        weigh_from_psum(0)
+        cast(q_bf, q_raw, 1)
+        quantize_k(1)
+        quantize_q(1)
+        shift_scales(1)
+        scores(1)
+        cast(v_bf, v_raw, 0)
+        weigh_from_sbuf(0)
+        quantize(v_codes[0][:], v_scales[0][:], v_bf[0][:])
+        quantize(p_codes[0][:], p_scales[0][:], p_bf[0][:])
+        values(0)
+        scalar_scores_out(1)
+        weigh_from_psum(1)
+        cast(v_bf, v_raw, 1)
+        weigh_from_sbuf(1)
+        quantize(v_codes[1][:], v_scales[1][:], v_bf[1][:])
+        quantize(p_codes[1][:], p_scales[1][:], p_bf[1][:])
+        norms(0, 0, 4)
+        values(1)
+        finish(0, 0, 4)
+        norms(1, 0, 2)
+        norms(1, 2, 4)
+        finish(1, 0, 2)
+        finish(1, 2, 4)

@@ -54,12 +54,12 @@ def tile_rows_win_rms_kernel(tc, kT, qT, dk, t, v, out):
         p_scales = tiles("p_scales", [P, W], U8)
         dkt = tiles("dkt", [P, PACK, W], F32)
         z_sb = tiles("z_sb", [P, W, PACK], F32)
+        squares = tiles("squares", [P, SIDE, W], F32)
         sq_sum = tiles("sq_sum", [P, SIDE], F32)
         rstd = tiles("rstd", [P, SIDE], F32)
         o_sb = tiles("o_sb", [P, SIDE, W], F32)
         dk_raw = sb.tile([P, PACK, W], F32, name="dk_raw")
         t_sb = sb.tile([P, SETS, PACK], F32, name="t_sb")
-        squares = sb.tile([P, W], F32, name="squares")
         warm_in = sb.tile([P, 1], F32, name="warm_in")
         warm_out = sb.tile([P, 1], F32, name="warm_out")
         banks = [[ps.tile([P, PACK, W], F32, name="bank%d_%d" % (u, g)) for g in range(SIDE)] for u in range(SETS)]
@@ -72,7 +72,7 @@ def tile_rows_win_rms_kernel(tc, kT, qT, dk, t, v, out):
 
         load(k_raw, kT, 0)
         load(q_raw, qT, 0)
-        nc.sync.dma_start(out=t_sb[:], in_=t.flatten_outer_dims().rearrange("(u p j) o -> p u (j o)", u=SETS, j=PACK))
+        nc.scalar.dma_start(out=t_sb[:], in_=t.flatten_outer_dims().rearrange("(u p j) o -> p u (j o)", u=SETS, j=PACK))
         for g in range(SIDE):
             nc.sync.dma_start(out=dk_raw[rows(g)], in_=dk.rearrange("(s r) q -> s r q", r=PACK))
         load(k_raw, kT, 1)
@@ -113,8 +113,8 @@ def tile_rows_win_rms_kernel(tc, kT, qT, dk, t, v, out):
             )
 
         def scores(u):
-            for step in (0, 2, 1, 3):
-                for g in range(SIDE):
+            for g in range(SIDE):
+                for step in (0, 2, 1, 3):
                     r = (g + step) % PACK
                     first = W + ROWS * (r - g)
                     if step % 2 == 0:
@@ -167,17 +167,19 @@ def tile_rows_win_rms_kernel(tc, kT, qT, dk, t, v, out):
                     stop=True,
                 )
 
-        def norms(u, lo, hi):
-            for g in range(lo, hi):
+        def square_sums(u, windows):
+            for g in windows:
                 nc.scalar.activation(
-                    out=squares[:], in_=banks[u][g][:, 0, :], func=ACT.Square, accum_out=sq_sum[u][:, g : g + 1]
+                    out=squares[u][:, g, :], in_=banks[u][g][:, 0, :], func=ACT.Square, accum_out=sq_sum[u][:, g : g + 1]
                 )
+
+        def inverse_rms(u, lo, hi):
             nc.scalar.activation(
                 out=rstd[u][:, lo:hi], in_=sq_sum[u][:, lo:hi], func=ACT.Abs_reciprocal_sqrt, scale=1.0 / E, bias=EPS
             )
 
-        def finish(u, lo, hi):
-            for g in range(lo, hi):
+        def normalize(u, windows):
+            for g in windows:
                 nc.vector.tensor_scalar(
                     out=o_sb[u][:, g, :],
                     in0=banks[u][g][:, 0, :],
@@ -185,6 +187,13 @@ def tile_rows_win_rms_kernel(tc, kT, qT, dk, t, v, out):
                     scalar2=None,
                     op0=ALU.mult,
                 )
+
+        def normalize_on_scalar(u, g):
+            nc.scalar.activation(
+                out=o_sb[u][:, g, :], in_=banks[u][g][:, 0, :], func=ACT.Copy, scale=rstd[u][:, g : g + 1]
+            )
+
+        def store(u, lo, hi):
             nc.sync.dma_start(out=out[SIDE * u + lo : SIDE * u + hi].rearrange("g q e -> q g e"), in_=o_sb[u][:, lo:hi, :])
 
         cast_k(0)
@@ -196,28 +205,35 @@ def tile_rows_win_rms_kernel(tc, kT, qT, dk, t, v, out):
         weights(0)
         weights(1)
         cast_k(1)
-        scalar_scores_out(0)
-        weigh_from_psum(0)
         cast(q_bf, q_raw, 1)
         quantize_k(1)
         quantize_q(1)
         shift_scales(1)
         scores(1)
+        scalar_scores_out(0)
         cast(v_bf, v_raw, 0)
+        cast(v_bf, v_raw, 1)
+        weigh_from_psum(0)
         weigh_from_sbuf(0)
         quantize(v_codes[0][:], v_scales[0][:], v_bf[0][:])
         quantize(p_codes[0][:], p_scales[0][:], p_bf[0][:])
         values(0)
         scalar_scores_out(1)
         weigh_from_psum(1)
-        cast(v_bf, v_raw, 1)
         weigh_from_sbuf(1)
         quantize(v_codes[1][:], v_scales[1][:], v_bf[1][:])
         quantize(p_codes[1][:], p_scales[1][:], p_bf[1][:])
-        norms(0, 0, 4)
+        square_sums(0, range(SIDE))
+        inverse_rms(0, 0, SIDE)
         values(1)
-        finish(0, 0, 4)
-        norms(1, 0, 2)
-        norms(1, 2, 4)
-        finish(1, 0, 2)
-        finish(1, 2, 4)
+        normalize(0, range(SIDE))
+        store(0, 0, SIDE)
+        square_sums(1, (0, 1, 2))
+        inverse_rms(1, 0, 2)
+        square_sums(1, (3,))
+        inverse_rms(1, 2, 4)
+        normalize(1, (0, 1))
+        store(1, 0, 2)
+        normalize(1, (2,))
+        normalize_on_scalar(1, 3)
+        store(1, 2, 4)

@@ -1,3 +1,4 @@
+import itertools
 from contextlib import ExitStack
 
 import concourse.mybir as mybir
@@ -21,7 +22,6 @@ SIDE = 4
 SETS = G // SIDE
 W = 128
 EPS = 1e-05
-SCALAR_WINDOWS = 3
 
 
 def tile_rows_win_rms_kernel(tc, kT, qT, dk, t, v, out):
@@ -113,8 +113,8 @@ def tile_rows_win_rms_kernel(tc, kT, qT, dk, t, v, out):
             )
 
         def scores(u):
-            for g in range(SIDE):
-                for step in (0, 2, 1, 3):
+            for pair, step, member in itertools.product(range(SIDE // 2), (0, 2, 1, 3), range(2)):
+                    g = 2 * pair + member
                     r = (g + step) % PACK
                     first = W + ROWS * (r - g)
                     if step % 2 == 0:
@@ -135,25 +135,20 @@ def tile_rows_win_rms_kernel(tc, kT, qT, dk, t, v, out):
             for r in range(PACK):
                 nc.scalar.activation(out=dkt[u][:, r, :], in_=dk_raw[:, r, :], func=ACT.Copy, scale=t_sb[:, u, r : r + 1])
 
-        def scalar_scores_out(u):
-            for g in range(SCALAR_WINDOWS):
+        def scores_out_scalar(u):
+            for g in range(1, SIDE):
                 nc.scalar.copy(out=z_sb[u][rows(g)], in_=banks[u][g][rows(g)].rearrange("p r q -> p q r"))
 
-        def weigh(u, part, z):
+        def scores_out_vector(u):
+            nc.vector.tensor_copy(out=z_sb[u][rows(0)], in_=banks[u][0][rows(0)].rearrange("p r q -> p q r"))
+
+        def weigh(u):
             nc.vector.tensor_tensor(
-                out=p_bf[u][part].rearrange("p (q r) -> p q r", r=PACK),
-                in0=z,
-                in1=dkt[u][part].rearrange("p r q -> p q r"),
+                out=p_bf[u][:].rearrange("p (q r) -> p q r", r=PACK),
+                in0=z_sb[u][:],
+                in1=dkt[u][:].rearrange("p r q -> p q r"),
                 op=ALU.mult,
             )
-
-        def weigh_from_psum(u):
-            for g in range(SCALAR_WINDOWS, SIDE):
-                weigh(u, rows(g), banks[u][g][rows(g)].rearrange("p r q -> p q r"))
-
-        def weigh_from_sbuf(u):
-            part = slice(0, ROWS * SCALAR_WINDOWS)
-            weigh(u, part, z_sb[u][part])
 
         def values(u):
             for g in range(SIDE):
@@ -210,18 +205,18 @@ def tile_rows_win_rms_kernel(tc, kT, qT, dk, t, v, out):
         quantize_q(1)
         shift_scales(1)
         scores(1)
-        scalar_scores_out(0)
+        scores_out_scalar(0)
+        scores_out_vector(0)
         cast(v_bf, v_raw, 0)
         cast(v_bf, v_raw, 1)
-        weigh_from_psum(0)
-        weigh_from_sbuf(0)
         quantize(v_codes[0][:], v_scales[0][:], v_bf[0][:])
+        weigh(0)
+        scores_out_scalar(1)
+        scores_out_vector(1)
         quantize(p_codes[0][:], p_scales[0][:], p_bf[0][:])
         values(0)
-        scalar_scores_out(1)
-        weigh_from_psum(1)
-        weigh_from_sbuf(1)
         quantize(v_codes[1][:], v_scales[1][:], v_bf[1][:])
+        weigh(1)
         quantize(p_codes[1][:], p_scales[1][:], p_bf[1][:])
         square_sums(0, range(SIDE))
         inverse_rms(0, 0, SIDE)

@@ -72,11 +72,11 @@ def tile_rows_win_rms_kernel(tc, kT, qT, dk, t, v, out):
 
         load(k_raw, kT, 0)
         load(q_raw, qT, 0)
+        load(k_raw, kT, 1)
+        load(q_raw, qT, 1)
         nc.scalar.dma_start(out=t_sb[:], in_=t.flatten_outer_dims().rearrange("(u p j) o -> p u (j o)", u=SETS, j=PACK))
         for g in range(SIDE):
             nc.sync.dma_start(out=dk_raw[rows(g)], in_=dk.rearrange("(s r) q -> s r q", r=PACK))
-        load(k_raw, kT, 1)
-        load(q_raw, qT, 1)
         load(v_raw, v, 0)
         load(v_raw, v, 1)
 
@@ -95,6 +95,11 @@ def tile_rows_win_rms_kernel(tc, kT, qT, dk, t, v, out):
 
         def cast(dst, src, u):
             nc.vector.tensor_copy(
+                out=dst[u][:].rearrange("p (c j) -> p c j", j=PACK), in_=src[u][:].rearrange("p j c -> p c j")
+            )
+
+        def cast_on_scalar(dst, src, u):
+            nc.scalar.copy(
                 out=dst[u][:].rearrange("p (c j) -> p c j", j=PACK), in_=src[u][:].rearrange("p j c -> p c j")
             )
 
@@ -133,7 +138,14 @@ def tile_rows_win_rms_kernel(tc, kT, qT, dk, t, v, out):
 
         def weights(u):
             for r in range(PACK):
-                nc.scalar.activation(out=dkt[u][:, r, :], in_=dk_raw[:, r, :], func=ACT.Copy, scale=t_sb[:, u, r : r + 1])
+                nc.gpsimd.tensor_scalar(
+                    out=dkt[u][:, r, :],
+                    in0=dk_raw[:, r, :],
+                    scalar1=t_sb[:, u, r : r + 1],
+                    scalar2=0.0,
+                    op0=ALU.mult,
+                    op1=ALU.add,
+                )
 
         def scores_out_scalar(u):
             for g in range(1, SIDE):
@@ -208,15 +220,15 @@ def tile_rows_win_rms_kernel(tc, kT, qT, dk, t, v, out):
         scores_out_scalar(0)
         scores_out_vector(0)
         cast(v_bf, v_raw, 0)
-        cast(v_bf, v_raw, 1)
-        quantize(v_codes[0][:], v_scales[0][:], v_bf[0][:])
-        weigh(0)
         scores_out_scalar(1)
         scores_out_vector(1)
+        weigh(0)
+        quantize(v_codes[0][:], v_scales[0][:], v_bf[0][:])
         quantize(p_codes[0][:], p_scales[0][:], p_bf[0][:])
         values(0)
-        quantize(v_codes[1][:], v_scales[1][:], v_bf[1][:])
+        cast_on_scalar(v_bf, v_raw, 1)
         weigh(1)
+        quantize(v_codes[1][:], v_scales[1][:], v_bf[1][:])
         quantize(p_codes[1][:], p_scales[1][:], p_bf[1][:])
         square_sums(0, range(SIDE))
         inverse_rms(0, 0, SIDE)

import itertools
from contextlib import ExitStack

import concourse.mybir as mybir

G, D, I, Q, E = 8, 128, 128, 128, 128
FLOPS = 2 * G * (D * I * Q + I * Q * E)

F32 = mybir.dt.float32
BF16 = mybir.dt.bfloat16
I32 = mybir.dt.int32
U32 = mybir.dt.uint32
U8 = mybir.dt.uint8
FP8X4 = mybir.dt.float8_e4m3fn_x4
ACT = mybir.ActivationFunctionType
ALU = mybir.AluOpType

P = 128
ROWS = 32
PACK = 4
SIDE = 4
SETS = G // SIDE
W = 128
EPS = 1e-05


def tile_rows_win_rms_kernel(tc, kT, qT, dk, t, v, out):
    nc = tc.nc

    def set_rows(x, u):
        return x.flatten_outer_dims()[u * P * PACK : (u + 1) * P * PACK, :].rearrange("(p j) c -> p j c", j=PACK)

    with ExitStack() as ctx:
        sb = ctx.enter_context(tc.tile_pool(name="sb", bufs=1))
        ps = ctx.enter_context(tc.psum_pool(name="ps", bufs=1))
        ctx.enter_context(tc.manual_schedule())

        def tiles(name, shape, dtype):
            return [sb.tile(shape, dtype, name="%s%d" % (name, u), align_bytes=64) for u in range(SETS)]

        k_raw = tiles("k_raw", [P, PACK, W], F32)
        q_raw = tiles("q_raw", [P, PACK, W], F32)
        v_raw = tiles("v_raw", [P, PACK, W], F32)
        k_bf = tiles("k_bf", [P, W * PACK], BF16)
        q_bf = tiles("q_bf", [P, W * PACK], BF16)
        v_bf = tiles("v_bf", [P, W * PACK], BF16)
        p_bf = tiles("p_bf", [P, W * PACK], BF16)
        kq_codes = tiles("kq_codes", [P, 3 * W], U32)
        kq_scales = tiles("kq_scales", [P, 3 * W], U8)
        odd_scales = tiles("odd_scales", [P, 3 * W], U8)
        v_codes = tiles("v_codes", [P, W], U32)
        v_scales = tiles("v_scales", [P, W], U8)
        p_codes = tiles("p_codes", [P, W], U32)
        p_scales = tiles("p_scales", [P, W], U8)
        dkt = tiles("dkt", [P, PACK, W], F32)
        z_sb = tiles("z_sb", [P, W, PACK], F32)
        squares = tiles("squares", [P, SIDE, W], F32)
        sq_sum = tiles("sq_sum", [P, SIDE], F32)
        rstd = tiles("rstd", [P, SIDE], F32)
        o_sb = tiles("o_sb", [P, SIDE, W], F32)
        dk_raw = sb.tile([P, PACK, W], F32, name="dk_raw")
        t_sb = sb.tile([P, SETS, PACK], F32, name="t_sb")
        warm_in = sb.tile([P, 1], F32, name="warm_in")
        warm_out = sb.tile([P, 1], F32, name="warm_out")
        banks = [[ps.tile([P, PACK, W], F32, name="bank%d_%d" % (u, g)) for g in range(SIDE)] for u in range(SETS)]

        def rows(g):
            return slice(ROWS * g, ROWS * (g + 1))

        def load(dst, x, u):
            nc.sync.dma_start(out=dst[u][:], in_=set_rows(x, u))

        load(k_raw, kT, 0)
        load(q_raw, qT, 0)
        load(k_raw, kT, 1)
        load(q_raw, qT, 1)
        nc.scalar.dma_start(out=t_sb[:], in_=t.flatten_outer_dims().rearrange("(u p j) o -> p u (j o)", u=SETS, j=PACK))
        for g in range(SIDE):
            nc.sync.dma_start(out=dk_raw[rows(g)], in_=dk.rearrange("(s r) q -> s r q", r=PACK))
        load(v_raw, v, 0)
        load(v_raw, v, 1)

        nc.vector.memset(warm_in[:], 1.0)
        nc.scalar.activation(out=warm_out[:], in_=warm_in[:], func=ACT.Abs_reciprocal_sqrt)
        for u in range(SETS):
            nc.vector.memset(kq_codes[u][:, 0:W].bitcast(I32), 0)
            nc.vector.memset(kq_scales[u][:, 0 : 2 * W].bitcast(I32), 0)
            nc.vector.memset(odd_scales[u][:].bitcast(I32), 0)

        def cast_k(u):
            nc.vector.tensor_copy(
                out=k_bf[u][:].rearrange("p (r s j) -> p s r j", r=PACK, j=PACK),
                in_=k_raw[u][:].rearrange("p j (s r) -> p s r j", r=PACK),
            )

        def cast(dst, src, u):
            nc.vector.tensor_copy(
                out=dst[u][:].rearrange("p (c j) -> p c j", j=PACK), in_=src[u][:].rearrange("p j c -> p c j")
            )

        def cast_on_scalar(dst, src, u):
            nc.scalar.copy(
                out=dst[u][:].rearrange("p (c j) -> p c j", j=PACK), in_=src[u][:].rearrange("p j c -> p c j")
            )

        def quantize(codes, scales, src):
            nc.vector.quantize_mx(out=codes.bitcast(FP8X4), scales=scales, in_=src)

        def quantize_k(u):
            quantize(kq_codes[u][:, W : 2 * W], kq_scales[u][:, W : 2 * W], k_bf[u][:])

        def quantize_q(u):
            quantize(kq_codes[u][:, 2 * W : 3 * W], kq_scales[u][:, 2 * W : 3 * W], q_bf[u][:])

        def shift_scales(u):
            nc.vector.tensor_copy(
                out=odd_scales[u][:, W + ROWS : 2 * W + ROWS].bitcast(I32), in_=kq_scales[u][:, W : 2 * W].bitcast(I32)
            )

        def scores(u):
            for pair, step, member in itertools.product(range(SIDE // 2), (0, 2, 1, 3), range(2)):
                    g = 2 * pair + member
                    r = (g + step) % PACK
                    first = W + ROWS * (r - g)
                    if step % 2 == 0:
                        k_scales = kq_scales[u][rows(g), first : first + W]
                    else:
                        k_scales = odd_scales[u][rows(g), first + ROWS : first + ROWS + W]
                    nc.tensor.matmul_mx(
                        out=banks[u][g][:, r, :],
                        lhsT=kq_codes[u][rows(g), first : first + W].bitcast(FP8X4),
                        lhsT_scale=k_scales,
                        rhs=kq_codes[u][rows(g), 2 * W : 3 * W].bitcast(FP8X4),
                        rhs_scale=kq_scales[u][rows(g), 2 * W : 3 * W],
                        start=True,
                        stop=True,
                    )

        def weights(u):
            for r in range(PACK):
                nc.gpsimd.tensor_scalar(
                    out=dkt[u][:, r, :],
                    in0=dk_raw[:, r, :],
                    scalar1=t_sb[:, u, r : r + 1],
                    scalar2=0.0,
                    op0=ALU.mult,
                    op1=ALU.add,
                )

        def scores_out_scalar(u):
            for g in range(1, SIDE):
                nc.scalar.copy(out=z_sb[u][rows(g)], in_=banks[u][g][rows(g)].rearrange("p r q -> p q r"))

        def scores_out_vector(u):
            nc.vector.tensor_copy(out=z_sb[u][rows(0)], in_=banks[u][0][rows(0)].rearrange("p r q -> p q r"))

        def weigh(u):
            nc.vector.tensor_tensor(
                out=p_bf[u][:].rearrange("p (q r) -> p q r", r=PACK),
                in0=z_sb[u][:],
                in1=dkt[u][:].rearrange("p r q -> p q r"),
                op=ALU.mult,
            )

        def values(u):
            for g in range(SIDE):
                nc.tensor.matmul_mx(
                    out=banks[u][g][:, 0, :],
                    lhsT=p_codes[u][rows(g), :].bitcast(FP8X4),
                    lhsT_scale=p_scales[u][rows(g), :],
                    rhs=v_codes[u][rows(g), :].bitcast(FP8X4),
                    rhs_scale=v_scales[u][rows(g), :],
                    start=True,
                    stop=True,
                )

        def square_sums(u, windows):
            for g in windows:
                nc.scalar.activation(
                    out=squares[u][:, g, :], in_=banks[u][g][:, 0, :], func=ACT.Square, accum_out=sq_sum[u][:, g : g + 1]
                )

        def inverse_rms(u, lo, hi):
            nc.scalar.activation(
                out=rstd[u][:, lo:hi], in_=sq_sum[u][:, lo:hi], func=ACT.Abs_reciprocal_sqrt, scale=1.0 / E, bias=EPS
            )

        def normalize(u, windows):
            for g in windows:
                nc.vector.tensor_scalar(
                    out=o_sb[u][:, g, :],
                    in0=banks[u][g][:, 0, :],
                    scalar1=rstd[u][:, g : g + 1],
                    scalar2=None,
                    op0=ALU.mult,
                )

        def normalize_on_scalar(u, g):
            nc.scalar.activation(
                out=o_sb[u][:, g, :], in_=banks[u][g][:, 0, :], func=ACT.Copy, scale=rstd[u][:, g : g + 1]
            )

        def store(u, lo, hi):
            nc.sync.dma_start(out=out[SIDE * u + lo : SIDE * u + hi].rearrange("g q e -> q g e"), in_=o_sb[u][:, lo:hi, :])

        cast_k(0)
        cast(q_bf, q_raw, 0)
        quantize_k(0)
        quantize_q(0)
        shift_scales(0)
        scores(0)
        weights(0)
        weights(1)
        cast_k(1)
        cast(q_bf, q_raw, 1)
        quantize_k(1)
        quantize_q(1)
        shift_scales(1)
        scores(1)
        scores_out_scalar(0)
        scores_out_vector(0)
        cast(v_bf, v_raw, 0)
        scores_out_scalar(1)
        scores_out_vector(1)
        weigh(0)
        quantize(v_codes[0][:], v_scales[0][:], v_bf[0][:])
        quantize(p_codes[0][:], p_scales[0][:], p_bf[0][:])
        values(0)
        cast_on_scalar(v_bf, v_raw, 1)
        weigh(1)
        quantize(v_codes[1][:], v_scales[1][:], v_bf[1][:])
        quantize(p_codes[1][:], p_scales[1][:], p_bf[1][:])
        square_sums(0, range(SIDE))
        inverse_rms(0, 0, SIDE)
        values(1)
        normalize(0, range(SIDE))
        store(0, 0, SIDE)
        square_sums(1, (0, 1, 2))
        inverse_rms(1, 0, 2)
        square_sums(1, (3,))
        inverse_rms(1, 2, 4)
        normalize(1, (0, 1))
        store(1, 0, 2)
        normalize(1, (2,))
        normalize_on_scalar(1, 3)
        store(1, 2, 4)
